import numpy as np
import ml_dtypes


def mxq(x, axis, fmt="e4m3"):
    dtype, down = {"e4m3": (ml_dtypes.float8_e4m3fn, 7), "e5m2": (ml_dtypes.float8_e5m2, 14)}[fmt]
    v = np.moveaxis(np.asarray(x, np.float32).astype(ml_dtypes.bfloat16).astype(np.float64), axis, -1)
    blocks = v.reshape(v.shape[:-1] + (-1, 32))
    amax = np.abs(blocks).max(-1, keepdims=True)
    byte = np.maximum(np.where(amax > 0, np.frexp(amax)[1] - 1 + 127, 0) - down, 1)
    scale = np.exp2(byte - 127.0)
    codes = (blocks / scale).astype(np.float32).astype(dtype).astype(np.float64)
    return np.moveaxis((codes * scale).reshape(v.shape), -1, axis)


WIDE = False


def mx_kscale(k):
    if not WIDE:
        return np.ones(k)
    levels = np.array([10, -10, 5, -5, 0])
    if k % 512:
        return np.exp2(np.random.permutation(np.resize(levels, k // 32))).repeat(32)
    a = np.empty((k // 512, 16))
    for p in range(k // 512):
        a[p, :8] = np.random.permutation(np.resize(levels, 8))
        for g in range(8):
            far = levels[np.abs(levels - a[p, g]) >= 10]
            a[p, g + 8] = far[np.random.randint(len(far))]
    return np.exp2(a.ravel()).repeat(32)


def f64(x):
    return np.asarray(x).astype(np.float64)


def striped8(idx):
    return np.asarray(idx).reshape(8, -1, 16).transpose(0, 2, 1).reshape(128, -1).astype(np.uint16)


def unstriped8(offs):
    return offs.reshape(8, 16, -1).transpose(0, 2, 1).reshape(8, -1).astype(np.int64)


def pick8(x, idx, run):
    r = np.arange(len(x))
    return x[r[:, None], idx[r % (8 * run) // run]]


E2M1 = np.array([0.0, 0.5, 1.0, 1.5, 2.0, 3.0, 4.0, 6.0, -0.0, -0.5, -1.0, -1.5, -2.0, -3.0, -4.0, -6.0])


def pack_weight(w, fmt):
    k, n = w.shape
    w = f64(np.asarray(w, np.float32).astype(ml_dtypes.bfloat16)).reshape(k // 32, 32, n)
    amax = np.abs(w).max(1)
    if fmt == "e4m3":
        byte = np.frexp(amax)[1] - 1 + 127 - 7
    else:
        mant, ex = np.frexp(amax / 6.0)
        byte = np.where(mant > 0.5, ex, ex - 1) + 127
    byte = np.clip(np.where(amax > 0, byte, 1), 1, 254)
    scaled = (w * np.exp2(127.0 - byte)[:, None, :]).reshape(k, n).astype(np.float32)
    by_word = np.ascontiguousarray(scaled.reshape(k // 512, 128, 4, n).transpose(0, 1, 3, 2))
    if fmt == "e4m3":
        words = by_word.astype(ml_dtypes.float8_e4m3fn).view(np.uint8)
    else:
        c = by_word.astype(ml_dtypes.float4_e2m1fn).view(np.uint8) & 0xF
        words = (c[..., 0::2] | (c[..., 1::2] << 4)).reshape(k // 512, 128, 2 * n)
    return np.ascontiguousarray(words), np.ascontiguousarray(byte.astype(np.uint8).reshape(k // 512, 16, n))


def unpack_weight(words, scales, fmt):
    g, _, n = scales.shape
    words = np.ascontiguousarray(words).reshape(g, 128, n, -1)
    if fmt == "e4m3":
        vals = words.view(ml_dtypes.float8_e4m3fn).astype(np.float64)
    else:
        nib = np.empty((g, 128, n, 4), np.uint8)
        nib[..., 0::2] = words & 0xF
        nib[..., 1::2] = words >> 4
        vals = E2M1[nib]
    vals = vals * np.repeat(np.exp2(scales.astype(np.float64) - 127.0), 8, axis=1)[..., None]
    return vals.transpose(0, 1, 3, 2).reshape(g * 512, n)


K, J, R, T, U, F, O, D, N, E = 512, 512, 512, 1024, 1024, 1024, 256, 1024, 256, 128


def setup_inputs():
    n = np.random.standard_normal
    idx = np.stack([np.random.permutation(T)[:J] for _ in range(8)])
    idx2 = np.stack([np.random.permutation(U)[:J] for _ in range(8)])
    idx3 = np.stack([np.random.permutation(F)[:R] for _ in range(8)])
    idx4 = np.stack([np.random.permutation(J)[:O] for _ in range(8)])
    idx5 = np.stack([np.random.permutation(D)[:O] for _ in range(8)])
    idx6 = np.stack([np.random.permutation(O)[:E] for _ in range(8)])
    idx7 = np.stack([np.random.permutation(O)[:E] for _ in range(8)])
    fk = mx_kscale(K)
    fr = mx_kscale(R)
    wbp = pack_weight(n((R, N)) * 1 / np.sqrt(R) / fr[:, None], "e2m1")
    wop = pack_weight(n((R, N)) * 1 / np.sqrt(R) / fr[:, None], "e4m3")
    return {
        "ta": (np.random.randint(-7, 8, (K, T)).astype(np.float64)).astype(np.float32),
        "tb": (np.random.randint(1, 9, (K, U)).astype(np.float64)).astype(np.float32),
        "ga": ((np.random.randint(8, 25, (K, 1)) / 64.0) * fk[:, None]).astype(np.float32),
        "gb": (np.random.uniform(0.1, 0.4, (K, 1))).astype(np.float32),
        "ua": (np.random.randint(-7, 8, (K, F)).astype(np.float64)).astype(np.float32),
        "ha": ((np.random.randint(8, 25, (K, 1)) / 1024.0) / fk[:, None]).astype(np.float32),
        "tl": (np.random.randint(-7, 8, (R, D)).astype(np.float64)).astype(np.float32),
        "sa": (np.random.uniform(0.5, 1.6, (R, 1)) * fr[:, None]).astype(np.float32),
        "sl": ((np.random.randint(6, 19, (R, 1)) / 64.0) * fr[:, None]).astype(np.float32),
        "wb_words": wbp[0],
        "wb_scales": wbp[1],
        "wo_words": wop[0],
        "wo_scales": wop[1],
        "so": (np.random.uniform(0.5, 1.6, (N, 1))).astype(np.float32),
        "sp": (np.random.uniform(0.5, 1.6, (N, 1))).astype(np.float32),
        "offs": striped8(idx),
        "offs2": striped8(idx2),
        "offs3": striped8(idx3),
        "offs4": striped8(idx4),
        "offs5": striped8(idx5),
        "offs6": striped8(idx6),
        "offs7": striped8(idx7),
    }


def reference(ta, tb, ga, gb, ua, ha, tl, sa, sl, wb_words, wb_scales, wo_words, wo_scales, so, sp, offs, offs2, offs3, offs4, offs5, offs6, offs7):
    idx = unstriped8(offs)
    idx2 = unstriped8(offs2)
    idx3 = unstriped8(offs3)
    idx4 = unstriped8(offs4)
    idx5 = unstriped8(offs5)
    idx6 = unstriped8(offs6)
    idx7 = unstriped8(offs7)
    wbu = unpack_weight(wb_words, wb_scales, "e2m1")
    wou = unpack_weight(wo_words, wo_scales, "e4m3")
    xc = pick8(f64(ta), idx, 64) * f64(ga) * pick8(f64(tb), idx2, 64) * f64(gb)
    wc = pick8(f64(ua), idx3, 64) * f64(ha)
    wcq = mxq(wc, 0, "e4m3")
    xcq = mxq(xc, 0, "e4m3")
    a = wcq.T @ xcq
    hid = np.maximum(pick8(a, idx4, 64) * f64(sa), pick8(f64(tl), idx5, 64) * f64(sl))
    hidq = mxq(hid, 0, "e4m3")
    p = wbu.T @ hidq
    q = wou.T @ hidq
    y = pick8(p, idx6, 16) * f64(so) - pick8(q, idx7, 16) * f64(sp)
    return y

@@ -1,0 +1,206 @@
+from contextlib import ExitStack
+
+import concourse.mybir as mybir
+
+F32 = mybir.dt.float32
+BF16 = mybir.dt.bfloat16
+I32 = mybir.dt.int32
+U32 = mybir.dt.uint32
+U16 = mybir.dt.uint16
+U8 = mybir.dt.uint8
+FP8X4 = mybir.dt.float8_e4m3fn_x4
+FP4X4 = mybir.dt.float4_e2m1fn_x4
+COPY = mybir.ActivationFunctionType.Copy
+ALU = mybir.AluOpType
+
+P = 128
+PACK = 4
+K, J, R, O, N, E = 512, 512, 512, 256, 256, 128
+TABLE = 1024
+LIST_ROWS = 16
+LINE = 4
+
+FLOPS = 2 * K * R * J + 2 * 2 * R * N * O
+
+
+def tile_picked_codegain_codes_one_codedlevel_outcomes_outmeet_kernel(
+    tc, ta, tb, ga, gb, ua, ha, tl, sa, sl, wb_words, wb_scales, wo_words, wo_scales, so, sp,
+    offs, offs2, offs3, offs4, offs5, offs6, offs7, out,
+):
+    nc = tc.nc
+    with ExitStack() as ctx:
+        keep = ctx.enter_context(tc.tile_pool(name="keep", bufs=1))
+        psum = ctx.enter_context(tc.psum_pool(name="psum", bufs=1))
+
+        def load_list(src, name):
+            t = keep.tile(list(src.shape), U16, name=name)
+            nc.sync.dma_start(t[:], src)
+            return t
+
+        def load_rows(src, t, name):
+            tile = keep.tile([P, TABLE], F32, name="%s%d" % (name, t))
+            nc.sync.dma_start(out=tile[:], in_=src.rearrange("(p t) c -> p t c", t=PACK)[:, t, :])
+            return tile
+
+        def load_steps(engine, src, name):
+            tile = keep.tile([P, PACK], F32, name=name)
+            engine.dma_start(out=tile[:], in_=src.rearrange("(p t) o -> p (t o)", t=PACK))
+            return tile
+
+        def load_out_weights(src, name):
+            tile = keep.tile([P, N // P], F32, name=name)
+            with nc.allow_non_contiguous_dma(reason="one value a partition"):
+                nc.sync.dma_start(out=tile[:], in_=src.rearrange("(b p) o -> p (b o)", p=P))
+            return tile
+
+        def load_scale_rows(src, name):
+            stage = keep.tile([4, 4, N // 4], I32, name=name + "_stage")
+            nc.sync.dma_start(out=stage[:], in_=src[0].bitcast(I32).rearrange("(q r) c -> r q c", r=4))
+            return stage
+
+        def spread_scale_rows(stage, name):
+            plane = keep.tile([P, N], U8, name=name, align_bytes=64)
+            nc.vector.memset(plane[:].bitcast(I32), 0)
+            for q in range(4):
+                nc.vector.tensor_copy(out=plane[32 * q : 32 * q + 4, :].bitcast(I32), in_=stage[:, q, :])
+            return plane
+
+        def gather(dst, window, offsets, start, count, scale):
+            cols = offsets[:, start // LIST_ROWS : (start + count) // LIST_ROWS]
+            nc.scalar.activation(out=dst, in_=window[:].indirect(cols), func=COPY, scale=scale)
+
+        def weave_pair(dst, in0, in1, u, c0, width, op):
+            o = dst[:, c0 : c0 + width, 2 * u : 2 * u + 2].rearrange("p (c i) t -> p c t i", i=LINE)
+            a = in0[:, :, c0 : c0 + width].rearrange("p t (c i) -> p c t i", i=LINE)
+            b = in1[:, :, c0 : c0 + width].rearrange("p t (c i) -> p c t i", i=LINE)
+            nc.vector.tensor_tensor(out=o, in0=a, in1=b, op=op)
+
+        ua_t, ta_t, tb_t, tl_t = [], [], [], []
+        ua_t.append(load_rows(ua, 0, "ua"))
+        l3 = load_list(offs3, "l3")
+        ha_t = load_steps(nc.scalar, ha, "ha_t")
+        ua_t.append(load_rows(ua, 1, "ua"))
+        ua_t.append(load_rows(ua, 2, "ua"))
+        l1 = load_list(offs, "l1")
+        ua_t.append(load_rows(ua, 3, "ua"))
+        ga_t = load_steps(nc.sync, ga, "ga_t")
+        ta_t.append(load_rows(ta, 0, "ta"))
+        l2 = load_list(offs2, "l2")
+        gb_t = load_steps(nc.sync, gb, "gb_t")
+        tb_t.append(load_rows(tb, 0, "tb"))
+        wb_stage = load_scale_rows(wb_scales, "wb")
+        ta_t.append(load_rows(ta, 1, "ta"))
+        wo_stage = load_scale_rows(wo_scales, "wo")
+        tb_t.append(load_rows(tb, 1, "tb"))
+        l5 = load_list(offs5, "l5")
+        ta_t.append(load_rows(ta, 2, "ta"))
+        sl_t = load_steps(nc.sync, sl, "sl_t")
+        tb_t.append(load_rows(tb, 2, "tb"))
+        l4 = load_list(offs4, "l4")
+        ta_t.append(load_rows(ta, 3, "ta"))
+        sa_t = load_steps(nc.sync, sa, "sa_t")
+        tb_t.append(load_rows(tb, 3, "tb"))
+        for t in range(PACK):
+            tl_t.append(load_rows(tl, t, "tl"))
+        wb_w = keep.tile([P, 2 * N], U8, name="wb_w", align_bytes=64)
+        nc.sync.dma_start(out=wb_w[:].bitcast(I32), in_=wb_words[0].bitcast(I32))
+        wo_w = keep.tile([P, N], U32, name="wo_w", align_bytes=64)
+        nc.sync.dma_start(out=wo_w[:].bitcast(I32), in_=wo_words[0].rearrange("p n t -> p (n t)").bitcast(I32))
+        l6 = load_list(offs6, "l6")
+        so_t = load_out_weights(so, "so_t")
+        l7 = load_list(offs7, "l7")
+        sp_t = load_out_weights(sp, "sp_t")
+
+        wb_s = spread_scale_rows(wb_stage, "wb_s")
+        wo_s = spread_scale_rows(wo_stage, "wo_s")
+
+        wg = keep.tile([P, PACK, R], BF16, name="wg")
+        for t in range(PACK):
+            gather(wg[:, t, :], ua_t[t], l3, 0, R, ha_t[:, t : t + 1])
+        wi = keep.tile([P, R * PACK], BF16, name="wi", align_bytes=64)
+        nc.vector.tensor_copy(
+            out=wi[:].rearrange("p (s m t) -> p s m t", s=PACK, t=PACK),
+            in_=wg[:].rearrange("p t (m s) -> p s m t", s=PACK),
+        )
+        wq = keep.tile([P, R], U32, name="wq", align_bytes=64)
+        wsc = keep.tile([P, R], U8, name="wsc", align_bytes=64)
+        nc.vector.quantize_mx(out=wq[:].bitcast(FP8X4), scales=wsc[:], in_=wi[:])
+
+        half_j = J // 2
+        xa = [keep.tile([P, 2, J], F32, name="xa%d" % u) for u in range(2)]
+        xb = [keep.tile([P, 2, J], F32, name="xb%d" % u) for u in range(2)]
+        xi = keep.tile([P, J, PACK], BF16, name="xi", align_bytes=64)
+        for t in range(PACK - 1):
+            gather(xa[t // 2][:, t % 2, :], ta_t[t], l1, 0, J, ga_t[:, t : t + 1])
+            gather(xb[t // 2][:, t % 2, :], tb_t[t], l2, 0, J, gb_t[:, t : t + 1])
+            if t == 1:
+                weave_pair(xi, xa[0], xb[0], 0, 0, J, ALU.mult)
+        a_sb = [keep.tile([P, J], F32, name="a%d" % s) for s in range(PACK)]
+        for h in range(2):
+            c0 = h * half_j
+            t = PACK - 1
+            gather(xa[1][:, 1, c0 : c0 + half_j], ta_t[t], l1, c0, half_j, ga_t[:, t : t + 1])
+            gather(xb[1][:, 1, c0 : c0 + half_j], tb_t[t], l2, c0, half_j, gb_t[:, t : t + 1])
+            weave_pair(xi, xa[1], xb[1], 1, c0, half_j, ALU.mult)
+            xq = keep.tile([P, half_j], U32, name="xq%d" % h, align_bytes=64)
+            xsc = keep.tile([P, half_j], U8, name="xsc%d" % h, align_bytes=64)
+            nc.vector.quantize_mx(
+                out=xq[:].bitcast(FP8X4), scales=xsc[:],
+                in_=xi[:, c0 : c0 + half_j, :].rearrange("p j t -> p (j t)"),
+            )
+            for sp2 in range(2):
+                bank = psum.tile([P, 2, half_j], F32, name="a_ps%d%d" % (h, sp2))
+                for i in range(2):
+                    s = 2 * sp2 + i
+                    nc.tensor.matmul_mx(
+                        out=bank[:, i, :],
+                        lhsT=wq[:, s * P : (s + 1) * P].bitcast(FP8X4), lhsT_scale=wsc[:, s * P : (s + 1) * P],
+                        rhs=xq[:].bitcast(FP8X4), rhs_scale=xsc[:], start=True, stop=True,
+                    )
+                for i in range(2):
+                    nc.vector.tensor_copy(out=a_sb[2 * sp2 + i][:, c0 : c0 + half_j], in_=bank[:, i, :])
+
+        half_o = O // 2
+        la = [keep.tile([P, 2, O], F32, name="la%d" % u) for u in range(2)]
+        lv = [keep.tile([P, 2, O], F32, name="lv%d" % u) for u in range(2)]
+        hi = keep.tile([P, O, PACK], BF16, name="hi", align_bytes=64)
+        for s in range(PACK):
+            gather(lv[s // 2][:, s % 2, :], tl_t[s], l5, 0, O, sl_t[:, s : s + 1])
+        p_sb = [keep.tile([P, O], F32, name="p%d" % b) for b in range(2)]
+        q_sb = [keep.tile([P, O], F32, name="q%d" % b) for b in range(2)]
+        for h in range(2):
+            c0 = h * half_o
+            for u in range(2):
+                for i in range(2):
+                    s = 2 * u + i
+                    gather(la[u][:, i, c0 : c0 + half_o], a_sb[s], l4, c0, half_o, sa_t[:, s : s + 1])
+                weave_pair(hi, la[u], lv[u], u, c0, half_o, ALU.max)
+            hq = keep.tile([P, half_o], U32, name="hq%d" % h, align_bytes=64)
+            hsc = keep.tile([P, half_o], U8, name="hsc%d" % h, align_bytes=64)
+            nc.vector.quantize_mx(
+                out=hq[:].bitcast(FP8X4), scales=hsc[:],
+                in_=hi[:, c0 : c0 + half_o, :].rearrange("p o t -> p (o t)"),
+            )
+            for b in range(2):
+                bank = psum.tile([P, 2, half_o], F32, name="pq_ps%d%d" % (h, b))
+                nc.tensor.matmul_mx(
+                    out=bank[:, 0, :],
+                    lhsT=wb_w[:, 2 * b * P : 2 * (b + 1) * P].bitcast(FP4X4), lhsT_scale=wb_s[:, b * P : (b + 1) * P],
+                    rhs=hq[:].bitcast(FP8X4), rhs_scale=hsc[:], start=True, stop=True,
+                )
+                nc.tensor.matmul_mx(
+                    out=bank[:, 1, :],
+                    lhsT=wo_w[:, b * P : (b + 1) * P].bitcast(FP8X4), lhsT_scale=wo_s[:, b * P : (b + 1) * P],
+                    rhs=hq[:].bitcast(FP8X4), rhs_scale=hsc[:], start=True, stop=True,
+                )
+                nc.vector.tensor_copy(out=p_sb[b][:, c0 : c0 + half_o], in_=bank[:, 0, :])
+                nc.vector.tensor_copy(out=q_sb[b][:, c0 : c0 + half_o], in_=bank[:, 1, :])
+
+        for b in range(2):
+            pg = keep.tile([P, E], F32, name="pg%d" % b)
+            qg = keep.tile([P, E], F32, name="qg%d" % b)
+            gather(pg[:], p_sb[b], l6, 0, E, so_t[:, b : b + 1])
+            gather(qg[:], q_sb[b], l7, 0, E, sp_t[:, b : b + 1])
+            y = keep.tile([P, E], F32, name="y%d" % b)
+            nc.vector.tensor_tensor(out=y[:], in0=pg[:], in1=qg[:], op=ALU.subtract)
+            nc.sync.dma_start(out=out[b * P : (b + 1) * P, :], in_=y[:])

@@ -136,6 +136,7 @@ def tile_picked_codegain_codes_one_codedlevel_outcomes_outmeet_kernel(
             if t == 1:
                 weave_pair(xi, xa[0], xb[0], 0, 0, J, ALU.mult)
         a_sb = [keep.tile([P, J], F32, name="a%d" % s) for s in range(PACK)]
+        a_ps = {}
         for h in range(2):
             c0 = h * half_j
             t = PACK - 1
@@ -148,59 +149,77 @@ def tile_picked_codegain_codes_one_codedlevel_outcomes_outmeet_kernel(
                 out=xq[:].bitcast(FP8X4), scales=xsc[:],
                 in_=xi[:, c0 : c0 + half_j, :].rearrange("p j t -> p (j t)"),
             )
-            for sp2 in range(2):
-                bank = psum.tile([P, 2, half_j], F32, name="a_ps%d%d" % (h, sp2))
-                for i in range(2):
-                    s = 2 * sp2 + i
-                    nc.tensor.matmul_mx(
-                        out=bank[:, i, :],
-                        lhsT=wq[:, s * P : (s + 1) * P].bitcast(FP8X4), lhsT_scale=wsc[:, s * P : (s + 1) * P],
-                        rhs=xq[:].bitcast(FP8X4), rhs_scale=xsc[:], start=True, stop=True,
-                    )
-                for i in range(2):
-                    nc.vector.tensor_copy(out=a_sb[2 * sp2 + i][:, c0 : c0 + half_j], in_=bank[:, i, :])
+            if h == 0:
+                pair = [psum.tile([P, 2, half_j], F32, name="a_first%d" % u, tag="bank%d" % u) for u in range(2)]
+                dst = [pair[s // 2][:, s % 2, :] for s in range(PACK)]
+            else:
+                dst = [psum.tile([P, half_j], F32, name="a_second%d" % s, tag="bank%d" % (2 + s))[:] for s in range(PACK)]
+            for s in range(PACK):
+                nc.tensor.matmul_mx(
+                    out=dst[s],
+                    lhsT=wq[:, s * P : (s + 1) * P].bitcast(FP8X4), lhsT_scale=wsc[:, s * P : (s + 1) * P],
+                    rhs=xq[:].bitcast(FP8X4), rhs_scale=xsc[:], start=True, stop=True,
+                )
+                a_ps[(h, s)] = dst[s]
+        for s in range(PACK):
+            for h in range(2):
+                nc.vector.tensor_copy(out=a_sb[s][:, h * half_j : (h + 1) * half_j], in_=a_ps[(h, s)])
 
         half_o = O // 2
-        la = [keep.tile([P, 2, O], F32, name="la%d" % u) for u in range(2)]
         lv = [keep.tile([P, 2, O], F32, name="lv%d" % u) for u in range(2)]
         hi = keep.tile([P, O, PACK], BF16, name="hi", align_bytes=64)
         for s in range(PACK):
             gather(lv[s // 2][:, s % 2, :], tl_t[s], l5, 0, O, sl_t[:, s : s + 1])
+        la = keep.tile([P, PACK, O], F32, name="la", tag="tl3")
         p_sb = [keep.tile([P, O], F32, name="p%d" % b) for b in range(2)]
         q_sb = [keep.tile([P, O], F32, name="q%d" % b) for b in range(2)]
+        hqs = []
         for h in range(2):
             c0 = h * half_o
             for u in range(2):
                 for i in range(2):
                     s = 2 * u + i
-                    gather(la[u][:, i, c0 : c0 + half_o], a_sb[s], l4, c0, half_o, sa_t[:, s : s + 1])
-                weave_pair(hi, la[u], lv[u], u, c0, half_o, ALU.max)
+                    gather(la[:, s, c0 : c0 + half_o], a_sb[s], l4, c0, half_o, sa_t[:, s : s + 1])
+                weave_pair(hi, la[:, 2 * u : 2 * u + 2, :], lv[u], u, c0, half_o, ALU.max)
             hq = keep.tile([P, half_o], U32, name="hq%d" % h, align_bytes=64)
             hsc = keep.tile([P, half_o], U8, name="hsc%d" % h, align_bytes=64)
             nc.vector.quantize_mx(
                 out=hq[:].bitcast(FP8X4), scales=hsc[:],
                 in_=hi[:, c0 : c0 + half_o, :].rearrange("p o t -> p (o t)"),
             )
-            for b in range(2):
-                bank = psum.tile([P, 2, half_o], F32, name="pq_ps%d%d" % (h, b))
-                nc.tensor.matmul_mx(
-                    out=bank[:, 0, :],
-                    lhsT=wb_w[:, 2 * b * P : 2 * (b + 1) * P].bitcast(FP4X4), lhsT_scale=wb_s[:, b * P : (b + 1) * P],
-                    rhs=hq[:].bitcast(FP8X4), rhs_scale=hsc[:], start=True, stop=True,
-                )
-                nc.tensor.matmul_mx(
-                    out=bank[:, 1, :],
-                    lhsT=wo_w[:, b * P : (b + 1) * P].bitcast(FP8X4), lhsT_scale=wo_s[:, b * P : (b + 1) * P],
-                    rhs=hq[:].bitcast(FP8X4), rhs_scale=hsc[:], start=True, stop=True,
-                )
-                nc.vector.tensor_copy(out=p_sb[b][:, c0 : c0 + half_o], in_=bank[:, 0, :])
-                nc.vector.tensor_copy(out=q_sb[b][:, c0 : c0 + half_o], in_=bank[:, 1, :])
+            hqs.append((hq, hsc))
+
+        def out_product(dst, h, b, second):
+            hq, hsc = hqs[h]
+            if second:
+                words, plane = wo_w[:, b * P : (b + 1) * P].bitcast(FP8X4), wo_s
+            else:
+                words, plane = wb_w[:, 2 * b * P : 2 * (b + 1) * P].bitcast(FP4X4), wb_s
+            nc.tensor.matmul_mx(
+                out=dst, lhsT=words, lhsT_scale=plane[:, b * P : (b + 1) * P],
+                rhs=hq[:].bitcast(FP8X4), rhs_scale=hsc[:], start=True, stop=True,
+            )
+
+        order = [(0, True), (0, False), (1, True), (1, False)]
+        first = psum.tile([P, 4, half_o], F32, name="pq_first", tag="bank6")
+        for i, (b, second) in enumerate(order):
+            out_product(first[:, i, :], 0, b, second)
+        for i, (b, second) in enumerate(order):
+            nc.scalar.copy(out=(q_sb if second else p_sb)[b][:, 0:half_o], in_=first[:, i, :])
+        for i, (b, second) in enumerate(order):
+            bank = psum.tile([P, half_o], F32, name="pq_second%d" % i, tag="bank%d" % ((7 + i) % 8))
+            out_product(bank[:], 1, b, second)
+            dst = (q_sb if second else p_sb)[b][:, half_o:O]
+            if i == 0:
+                nc.scalar.copy(out=dst, in_=bank[:])
+            else:
+                nc.vector.tensor_copy(out=dst, in_=bank[:])
 
         for b in range(2):
             pg = keep.tile([P, E], F32, name="pg%d" % b)
             qg = keep.tile([P, E], F32, name="qg%d" % b)
-            gather(pg[:], p_sb[b], l6, 0, E, so_t[:, b : b + 1])
             gather(qg[:], q_sb[b], l7, 0, E, sp_t[:, b : b + 1])
+            gather(pg[:], p_sb[b], l6, 0, E, so_t[:, b : b + 1])
             y = keep.tile([P, E], F32, name="y%d" % b)
             nc.vector.tensor_tensor(out=y[:], in0=pg[:], in1=qg[:], op=ALU.subtract)
             nc.sync.dma_start(out=out[b * P : (b + 1) * P, :], in_=y[:])

@@ -75,6 +75,11 @@ def tile_picked_codegain_codes_one_codedlevel_outcomes_outmeet_kernel(
             b = in1[:, :, c0 : c0 + width].rearrange("p t (c i) -> p c t i", i=LINE)
             nc.vector.tensor_tensor(out=o, in0=a, in1=b, op=op)
 
+        warm = keep.tile([P, 8], F32, name="warm")
+        nc.vector.memset(warm[:], 0.0)
+        warm_out = keep.tile([P, 8], F32, name="warm_out")
+        nc.scalar.activation(out=warm_out[:], in_=warm[:], func=COPY)
+
         ua_t, ta_t, tb_t, tl_t = [], [], [], []
         ua_t.append(load_rows(ua, 0, "ua"))
         l3 = load_list(offs3, "l3")

@@ -85,28 +85,29 @@ def tile_picked_codegain_codes_one_codedlevel_outcomes_outmeet_kernel(
         l3 = load_list(offs3, "l3")
         ha_t = load_steps(nc.scalar, ha, "ha_t")
         ua_t.append(load_rows(ua, 1, "ua"))
+        wb_stage = load_scale_rows(wb_scales, "wb")
         ua_t.append(load_rows(ua, 2, "ua"))
         l1 = load_list(offs, "l1")
         ua_t.append(load_rows(ua, 3, "ua"))
         ga_t = load_steps(nc.sync, ga, "ga_t")
+        wo_stage = load_scale_rows(wo_scales, "wo")
         ta_t.append(load_rows(ta, 0, "ta"))
         l2 = load_list(offs2, "l2")
         gb_t = load_steps(nc.sync, gb, "gb_t")
         tb_t.append(load_rows(tb, 0, "tb"))
-        wb_stage = load_scale_rows(wb_scales, "wb")
-        ta_t.append(load_rows(ta, 1, "ta"))
-        wo_stage = load_scale_rows(wo_scales, "wo")
-        tb_t.append(load_rows(tb, 1, "tb"))
+        for t in range(1, PACK):
+            ta_t.append(load_rows(ta, t, "ta"))
+            tb_t.append(load_rows(tb, t, "tb"))
+        tl_t.append(load_rows(tl, 0, "tl"))
+        ga_last = keep.tile([P, 1], F32, name="ga_last")
+        with nc.allow_non_contiguous_dma(reason="one value a partition"):
+            nc.sync.dma_start(out=ga_last[:], in_=ga.rearrange("(p t) o -> p (t o)", t=PACK)[:, PACK - 1 : PACK])
         l5 = load_list(offs5, "l5")
-        ta_t.append(load_rows(ta, 2, "ta"))
         sl_t = load_steps(nc.sync, sl, "sl_t")
-        tb_t.append(load_rows(tb, 2, "tb"))
-        l4 = load_list(offs4, "l4")
-        ta_t.append(load_rows(ta, 3, "ta"))
-        sa_t = load_steps(nc.sync, sa, "sa_t")
-        tb_t.append(load_rows(tb, 3, "tb"))
-        for t in range(PACK):
+        for t in range(1, PACK):
             tl_t.append(load_rows(tl, t, "tl"))
+        l4 = load_list(offs4, "l4")
+        sa_t = load_steps(nc.sync, sa, "sa_t")
         wb_w = keep.tile([P, 2 * N], U8, name="wb_w", align_bytes=64)
         nc.sync.dma_start(out=wb_w[:].bitcast(I32), in_=wb_words[0].bitcast(I32))
         wo_w = keep.tile([P, N], U32, name="wo_w", align_bytes=64)
@@ -140,12 +141,12 @@ def tile_picked_codegain_codes_one_codedlevel_outcomes_outmeet_kernel(
             gather(xb[t // 2][:, t % 2, :], tb_t[t], l2, 0, J, gb_t[:, t : t + 1])
             if t == 1:
                 weave_pair(xi, xa[0], xb[0], 0, 0, J, ALU.mult)
-        a_sb = [keep.tile([P, J], F32, name="a%d" % s) for s in range(PACK)]
         a_ps = {}
+        a1_ps = psum.tile([P, J], F32, name="a1_ps", tag="bank1")
         for h in range(2):
             c0 = h * half_j
             t = PACK - 1
-            gather(xa[1][:, 1, c0 : c0 + half_j], ta_t[t], l1, c0, half_j, ga_t[:, t : t + 1])
+            gather(xa[1][:, 1, c0 : c0 + half_j], ta_t[t], l1, c0, half_j, ga_t[:, t : t + 1] if h == 0 else ga_last[:])
             gather(xb[1][:, 1, c0 : c0 + half_j], tb_t[t], l2, c0, half_j, gb_t[:, t : t + 1])
             weave_pair(xi, xa[1], xb[1], 1, c0, half_j, ALU.mult)
             xq = keep.tile([P, half_j], U32, name="xq%d" % h, align_bytes=64)
@@ -154,11 +155,11 @@ def tile_picked_codegain_codes_one_codedlevel_outcomes_outmeet_kernel(
                 out=xq[:].bitcast(FP8X4), scales=xsc[:],
                 in_=xi[:, c0 : c0 + half_j, :].rearrange("p j t -> p (j t)"),
             )
-            if h == 0:
-                pair = [psum.tile([P, 2, half_j], F32, name="a_first%d" % u, tag="bank%d" % u) for u in range(2)]
-                dst = [pair[s // 2][:, s % 2, :] for s in range(PACK)]
-            else:
-                dst = [psum.tile([P, half_j], F32, name="a_second%d" % s, tag="bank%d" % (2 + s))[:] for s in range(PACK)]
+            dst = [
+                a1_ps[:, c0 : c0 + half_j] if s == 1
+                else psum.tile([P, half_j], F32, name="a_ps%d%d" % (h, s), tag="bank%d" % (PACK * h + s))[:]
+                for s in range(PACK)
+            ]
             for s in range(PACK):
                 nc.tensor.matmul_mx(
                     out=dst[s],
@@ -166,7 +167,16 @@ def tile_picked_codegain_codes_one_codedlevel_outcomes_outmeet_kernel(
                     rhs=xq[:].bitcast(FP8X4), rhs_scale=xsc[:], start=True, stop=True,
                 )
                 a_ps[(h, s)] = dst[s]
+        a_sb = [
+            keep.tile([P, J], F32, name="a0", tag="xa1"),
+            keep.tile([P, J], F32, name="a1"),
+            keep.tile([P, J], F32, name="a2", tag="xb1"),
+            keep.tile([P, J], F32, name="a3", tag="xi", align_bytes=64),
+        ]
         for s in range(PACK):
+            if s == 1:
+                nc.vector.tensor_copy(out=a_sb[s][:], in_=a1_ps[:])
+                continue
             for h in range(2):
                 nc.vector.tensor_copy(out=a_sb[s][:, h * half_j : (h + 1) * half_j], in_=a_ps[(h, s)])
 
@@ -175,50 +185,46 @@ def tile_picked_codegain_codes_one_codedlevel_outcomes_outmeet_kernel(
         hi = keep.tile([P, O, PACK], BF16, name="hi", align_bytes=64)
         for s in range(PACK):
             gather(lv[s // 2][:, s % 2, :], tl_t[s], l5, 0, O, sl_t[:, s : s + 1])
-        la = keep.tile([P, PACK, O], F32, name="la", tag="tl3")
+        la = keep.tile([P, PACK, O], F32, name="la")
         p_sb = [keep.tile([P, O], F32, name="p%d" % b) for b in range(2)]
         q_sb = [keep.tile([P, O], F32, name="q%d" % b) for b in range(2)]
-        hqs = []
+        for s in range(2):
+            gather(la[:, s, :], a_sb[s], l4, 0, O, sa_t[:, s : s + 1])
+        for h in range(2):
+            weave_pair(hi, la[:, 0:2, :], lv[0], 0, h * half_o, half_o, ALU.max)
         for h in range(2):
             c0 = h * half_o
-            for u in range(2):
-                for i in range(2):
-                    s = 2 * u + i
-                    gather(la[:, s, c0 : c0 + half_o], a_sb[s], l4, c0, half_o, sa_t[:, s : s + 1])
-                weave_pair(hi, la[:, 2 * u : 2 * u + 2, :], lv[u], u, c0, half_o, ALU.max)
-            hq = keep.tile([P, half_o], U32, name="hq%d" % h, align_bytes=64)
-            hsc = keep.tile([P, half_o], U8, name="hsc%d" % h, align_bytes=64)
+            for s in range(2, PACK):
+                gather(la[:, s, c0 : c0 + half_o], a_sb[s], l4, c0, half_o, sa_t[:, s : s + 1])
+            weave_pair(hi, la[:, 2:4, :], lv[1], 1, c0, half_o, ALU.max)
+        hq = keep.tile([P, O], U32, name="hq", align_bytes=64)
+        hsc = keep.tile([P, O], U8, name="hsc", align_bytes=64)
+        for h in range(2):
+            cols = slice(h * half_o, (h + 1) * half_o)
             nc.vector.quantize_mx(
-                out=hq[:].bitcast(FP8X4), scales=hsc[:],
-                in_=hi[:, c0 : c0 + half_o, :].rearrange("p o t -> p (o t)"),
+                out=hq[:, cols].bitcast(FP8X4), scales=hsc[:, cols],
+                in_=hi[:, cols, :].rearrange("p o t -> p (o t)"),
             )
-            hqs.append((hq, hsc))
 
-        def out_product(dst, h, b, second):
-            hq, hsc = hqs[h]
+        def out_product(dst, cols, b, second):
             if second:
                 words, plane = wo_w[:, b * P : (b + 1) * P].bitcast(FP8X4), wo_s
             else:
                 words, plane = wb_w[:, 2 * b * P : 2 * (b + 1) * P].bitcast(FP4X4), wb_s
             nc.tensor.matmul_mx(
                 out=dst, lhsT=words, lhsT_scale=plane[:, b * P : (b + 1) * P],
-                rhs=hq[:].bitcast(FP8X4), rhs_scale=hsc[:], start=True, stop=True,
+                rhs=hq[:, cols].bitcast(FP8X4), rhs_scale=hsc[:, cols], start=True, stop=True,
             )
 
-        order = [(0, True), (0, False), (1, True), (1, False)]
-        first = psum.tile([P, 4, half_o], F32, name="pq_first", tag="bank6")
-        for i, (b, second) in enumerate(order):
-            out_product(first[:, i, :], 0, b, second)
-        for i, (b, second) in enumerate(order):
-            nc.scalar.copy(out=(q_sb if second else p_sb)[b][:, 0:half_o], in_=first[:, i, :])
-        for i, (b, second) in enumerate(order):
-            bank = psum.tile([P, half_o], F32, name="pq_second%d" % i, tag="bank%d" % ((7 + i) % 8))
-            out_product(bank[:], 1, b, second)
-            dst = (q_sb if second else p_sb)[b][:, half_o:O]
-            if i == 0:
-                nc.scalar.copy(out=dst, in_=bank[:])
-            else:
-                nc.vector.tensor_copy(out=dst, in_=bank[:])
+        for h in range(2):
+            cols = slice(h * half_o, (h + 1) * half_o)
+            bank = psum.tile([P, half_o], F32, name="q0_ps%d" % h, tag="bank%d" % (2 + h))
+            out_product(bank[:], cols, 0, True)
+            nc.scalar.copy(out=q_sb[0][:, cols], in_=bank[:])
+        for i, (b, second) in enumerate([(0, False), (1, True), (1, False)]):
+            bank = psum.tile([P, O], F32, name="pq_ps%d" % i, tag="bank%d" % (i if i < 2 else 4))
+            out_product(bank[:], slice(0, O), b, second)
+            nc.vector.tensor_copy(out=(q_sb if second else p_sb)[b][:], in_=bank[:])
 
         for b in range(2):
             pg = keep.tile([P, E], F32, name="pg%d" % b)

from contextlib import ExitStack

import concourse.mybir as mybir

F32 = mybir.dt.float32
BF16 = mybir.dt.bfloat16
I32 = mybir.dt.int32
U32 = mybir.dt.uint32
U16 = mybir.dt.uint16
U8 = mybir.dt.uint8
FP8X4 = mybir.dt.float8_e4m3fn_x4
FP4X4 = mybir.dt.float4_e2m1fn_x4
COPY = mybir.ActivationFunctionType.Copy
ALU = mybir.AluOpType

P = 128
PACK = 4
K, J, R, O, N, E = 512, 512, 512, 256, 256, 128
TABLE = 1024
LIST_ROWS = 16
LINE = 4

FLOPS = 2 * K * R * J + 2 * 2 * R * N * O


def tile_picked_codegain_codes_one_codedlevel_outcomes_outmeet_kernel(
    tc, ta, tb, ga, gb, ua, ha, tl, sa, sl, wb_words, wb_scales, wo_words, wo_scales, so, sp,
    offs, offs2, offs3, offs4, offs5, offs6, offs7, out,
):
    nc = tc.nc
    with ExitStack() as ctx:
        keep = ctx.enter_context(tc.tile_pool(name="keep", bufs=1))
        psum = ctx.enter_context(tc.psum_pool(name="psum", bufs=1))

        def load_list(src, name):
            t = keep.tile(list(src.shape), U16, name=name)
            nc.sync.dma_start(t[:], src)
            return t

        def load_rows(src, t, name):
            tile = keep.tile([P, TABLE], F32, name="%s%d" % (name, t))
            nc.sync.dma_start(out=tile[:], in_=src.rearrange("(p t) c -> p t c", t=PACK)[:, t, :])
            return tile

        def load_steps(engine, src, name):
            tile = keep.tile([P, PACK], F32, name=name)
            engine.dma_start(out=tile[:], in_=src.rearrange("(p t) o -> p (t o)", t=PACK))
            return tile

        def load_out_weights(src, name):
            tile = keep.tile([P, N // P], F32, name=name)
            with nc.allow_non_contiguous_dma(reason="one value a partition"):
                nc.sync.dma_start(out=tile[:], in_=src.rearrange("(b p) o -> p (b o)", p=P))
            return tile

        def load_scale_rows(src, name):
            stage = keep.tile([4, 4, N // 4], I32, name=name + "_stage")
            nc.sync.dma_start(out=stage[:], in_=src[0].bitcast(I32).rearrange("(q r) c -> r q c", r=4))
            return stage

        def spread_scale_rows(stage, name):
            plane = keep.tile([P, N], U8, name=name, align_bytes=64)
            nc.vector.memset(plane[:].bitcast(I32), 0)
            for q in range(4):
                nc.vector.tensor_copy(out=plane[32 * q : 32 * q + 4, :].bitcast(I32), in_=stage[:, q, :])
            return plane

        def gather(dst, window, offsets, start, count, scale):
            cols = offsets[:, start // LIST_ROWS : (start + count) // LIST_ROWS]
            nc.scalar.activation(out=dst, in_=window[:].indirect(cols), func=COPY, scale=scale)

        def weave_pair(dst, in0, in1, u, c0, width, op):
            o = dst[:, c0 : c0 + width, 2 * u : 2 * u + 2].rearrange("p (c i) t -> p c t i", i=LINE)
            a = in0[:, :, c0 : c0 + width].rearrange("p t (c i) -> p c t i", i=LINE)
            b = in1[:, :, c0 : c0 + width].rearrange("p t (c i) -> p c t i", i=LINE)
            nc.vector.tensor_tensor(out=o, in0=a, in1=b, op=op)

        warm = keep.tile([P, 8], F32, name="warm")
        nc.vector.memset(warm[:], 0.0)
        warm_out = keep.tile([P, 8], F32, name="warm_out")
        nc.scalar.activation(out=warm_out[:], in_=warm[:], func=COPY)

        ua_t, ta_t, tb_t, tl_t = [], [], [], []
        ua_t.append(load_rows(ua, 0, "ua"))
        l3 = load_list(offs3, "l3")
        ha_t = load_steps(nc.scalar, ha, "ha_t")
        ua_t.append(load_rows(ua, 1, "ua"))
        wb_stage = load_scale_rows(wb_scales, "wb")
        ua_t.append(load_rows(ua, 2, "ua"))
        l1 = load_list(offs, "l1")
        ua_t.append(load_rows(ua, 3, "ua"))
        ga_t = load_steps(nc.sync, ga, "ga_t")
        wo_stage = load_scale_rows(wo_scales, "wo")
        ta_t.append(load_rows(ta, 0, "ta"))
        l2 = load_list(offs2, "l2")
        gb_t = load_steps(nc.sync, gb, "gb_t")
        tb_t.append(load_rows(tb, 0, "tb"))
        for t in range(1, PACK):
            ta_t.append(load_rows(ta, t, "ta"))
            tb_t.append(load_rows(tb, t, "tb"))
        tl_t.append(load_rows(tl, 0, "tl"))
        ga_last = keep.tile([P, 1], F32, name="ga_last")
        with nc.allow_non_contiguous_dma(reason="one value a partition"):
            nc.sync.dma_start(out=ga_last[:], in_=ga.rearrange("(p t) o -> p (t o)", t=PACK)[:, PACK - 1 : PACK])
        l5 = load_list(offs5, "l5")
        sl_t = load_steps(nc.sync, sl, "sl_t")
        for t in range(1, PACK):
            tl_t.append(load_rows(tl, t, "tl"))
        l4 = load_list(offs4, "l4")
        sa_t = load_steps(nc.sync, sa, "sa_t")
        wb_w = keep.tile([P, 2 * N], U8, name="wb_w", align_bytes=64)
        nc.sync.dma_start(out=wb_w[:].bitcast(I32), in_=wb_words[0].bitcast(I32))
        wo_w = keep.tile([P, N], U32, name="wo_w", align_bytes=64)
        nc.sync.dma_start(out=wo_w[:].bitcast(I32), in_=wo_words[0].rearrange("p n t -> p (n t)").bitcast(I32))
        l6 = load_list(offs6, "l6")
        so_t = load_out_weights(so, "so_t")
        l7 = load_list(offs7, "l7")
        sp_t = load_out_weights(sp, "sp_t")

        wb_s = spread_scale_rows(wb_stage, "wb_s")
        wo_s = spread_scale_rows(wo_stage, "wo_s")

        wg = keep.tile([P, PACK, R], BF16, name="wg")
        for t in range(PACK):
            gather(wg[:, t, :], ua_t[t], l3, 0, R, ha_t[:, t : t + 1])
        wi = keep.tile([P, R * PACK], BF16, name="wi", align_bytes=64)
        nc.vector.tensor_copy(
            out=wi[:].rearrange("p (s m t) -> p s m t", s=PACK, t=PACK),
            in_=wg[:].rearrange("p t (m s) -> p s m t", s=PACK),
        )
        wq = keep.tile([P, R], U32, name="wq", align_bytes=64)
        wsc = keep.tile([P, R], U8, name="wsc", align_bytes=64)
        nc.vector.quantize_mx(out=wq[:].bitcast(FP8X4), scales=wsc[:], in_=wi[:])

        half_j = J // 2
        xa = [keep.tile([P, 2, J], F32, name="xa%d" % u) for u in range(2)]
        xb = [keep.tile([P, 2, J], F32, name="xb%d" % u) for u in range(2)]
        xi = keep.tile([P, J, PACK], BF16, name="xi", align_bytes=64)
        for t in range(PACK - 1):
            gather(xa[t // 2][:, t % 2, :], ta_t[t], l1, 0, J, ga_t[:, t : t + 1])
            gather(xb[t // 2][:, t % 2, :], tb_t[t], l2, 0, J, gb_t[:, t : t + 1])
            if t == 1:
                weave_pair(xi, xa[0], xb[0], 0, 0, J, ALU.mult)
        a_ps = {}
        a1_ps = psum.tile([P, J], F32, name="a1_ps", tag="bank1")
        for h in range(2):
            c0 = h * half_j
            t = PACK - 1
            gather(xa[1][:, 1, c0 : c0 + half_j], ta_t[t], l1, c0, half_j, ga_t[:, t : t + 1] if h == 0 else ga_last[:])
            gather(xb[1][:, 1, c0 : c0 + half_j], tb_t[t], l2, c0, half_j, gb_t[:, t : t + 1])
            weave_pair(xi, xa[1], xb[1], 1, c0, half_j, ALU.mult)
            xq = keep.tile([P, half_j], U32, name="xq%d" % h, align_bytes=64)
            xsc = keep.tile([P, half_j], U8, name="xsc%d" % h, align_bytes=64)
            nc.vector.quantize_mx(
                out=xq[:].bitcast(FP8X4), scales=xsc[:],
                in_=xi[:, c0 : c0 + half_j, :].rearrange("p j t -> p (j t)"),
            )
            dst = [
                a1_ps[:, c0 : c0 + half_j] if s == 1
                else psum.tile([P, half_j], F32, name="a_ps%d%d" % (h, s), tag="bank%d" % (PACK * h + s))[:]
                for s in range(PACK)
            ]
            for s in range(PACK):
                nc.tensor.matmul_mx(
                    out=dst[s],
                    lhsT=wq[:, s * P : (s + 1) * P].bitcast(FP8X4), lhsT_scale=wsc[:, s * P : (s + 1) * P],
                    rhs=xq[:].bitcast(FP8X4), rhs_scale=xsc[:], start=True, stop=True,
                )
                a_ps[(h, s)] = dst[s]
        a_sb = [
            keep.tile([P, J], F32, name="a0", tag="xa1"),
            keep.tile([P, J], F32, name="a1"),
            keep.tile([P, J], F32, name="a2", tag="xb1"),
            keep.tile([P, J], F32, name="a3", tag="xi", align_bytes=64),
        ]
        for s in range(PACK):
            if s == 1:
                nc.vector.tensor_copy(out=a_sb[s][:], in_=a1_ps[:])
                continue
            for h in range(2):
                nc.vector.tensor_copy(out=a_sb[s][:, h * half_j : (h + 1) * half_j], in_=a_ps[(h, s)])

        half_o = O // 2
        lv = [keep.tile([P, 2, O], F32, name="lv%d" % u) for u in range(2)]
        hi = keep.tile([P, O, PACK], BF16, name="hi", align_bytes=64)
        for s in range(PACK):
            gather(lv[s // 2][:, s % 2, :], tl_t[s], l5, 0, O, sl_t[:, s : s + 1])
        la = keep.tile([P, PACK, O], F32, name="la")
        p_sb = [keep.tile([P, O], F32, name="p%d" % b) for b in range(2)]
        q_sb = [keep.tile([P, O], F32, name="q%d" % b) for b in range(2)]
        for s in range(2):
            gather(la[:, s, :], a_sb[s], l4, 0, O, sa_t[:, s : s + 1])
        for h in range(2):
            weave_pair(hi, la[:, 0:2, :], lv[0], 0, h * half_o, half_o, ALU.max)
        for h in range(2):
            c0 = h * half_o
            for s in range(2, PACK):
                gather(la[:, s, c0 : c0 + half_o], a_sb[s], l4, c0, half_o, sa_t[:, s : s + 1])
            weave_pair(hi, la[:, 2:4, :], lv[1], 1, c0, half_o, ALU.max)
        hq = keep.tile([P, O], U32, name="hq", align_bytes=64)
        hsc = keep.tile([P, O], U8, name="hsc", align_bytes=64)
        for h in range(2):
            cols = slice(h * half_o, (h + 1) * half_o)
            nc.vector.quantize_mx(
                out=hq[:, cols].bitcast(FP8X4), scales=hsc[:, cols],
                in_=hi[:, cols, :].rearrange("p o t -> p (o t)"),
            )

        def out_product(dst, cols, b, second):
            if second:
                words, plane = wo_w[:, b * P : (b + 1) * P].bitcast(FP8X4), wo_s
            else:
                words, plane = wb_w[:, 2 * b * P : 2 * (b + 1) * P].bitcast(FP4X4), wb_s
            nc.tensor.matmul_mx(
                out=dst, lhsT=words, lhsT_scale=plane[:, b * P : (b + 1) * P],
                rhs=hq[:, cols].bitcast(FP8X4), rhs_scale=hsc[:, cols], start=True, stop=True,
            )

        for h in range(2):
            cols = slice(h * half_o, (h + 1) * half_o)
            bank = psum.tile([P, half_o], F32, name="q0_ps%d" % h, tag="bank%d" % (2 + h))
            out_product(bank[:], cols, 0, True)
            nc.scalar.copy(out=q_sb[0][:, cols], in_=bank[:])
        for i, (b, second) in enumerate([(0, False), (1, True), (1, False)]):
            bank = psum.tile([P, O], F32, name="pq_ps%d" % i, tag="bank%d" % (i if i < 2 else 4))
            out_product(bank[:], slice(0, O), b, second)
            nc.vector.tensor_copy(out=(q_sb if second else p_sb)[b][:], in_=bank[:])

        for b in range(2):
            pg = keep.tile([P, E], F32, name="pg%d" % b)
            qg = keep.tile([P, E], F32, name="qg%d" % b)
            gather(qg[:], q_sb[b], l7, 0, E, sp_t[:, b : b + 1])
            gather(pg[:], p_sb[b], l6, 0, E, so_t[:, b : b + 1])
            y = keep.tile([P, E], F32, name="y%d" % b)
            nc.vector.tensor_tensor(out=y[:], in0=pg[:], in1=qg[:], op=ALU.subtract)
            nc.sync.dma_start(out=out[b * P : (b + 1) * P, :], in_=y[:])
